import numpy as np
import ml_dtypes


def mxq(x, axis, fmt="e4m3"):
    dtype, down = {"e4m3": (ml_dtypes.float8_e4m3fn, 7), "e5m2": (ml_dtypes.float8_e5m2, 14)}[fmt]
    v = np.moveaxis(np.asarray(x, np.float32).astype(ml_dtypes.bfloat16).astype(np.float64), axis, -1)
    blocks = v.reshape(v.shape[:-1] + (-1, 32))
    amax = np.abs(blocks).max(-1, keepdims=True)
    byte = np.maximum(np.where(amax > 0, np.frexp(amax)[1] - 1 + 127, 0) - down, 1)
    scale = np.exp2(byte - 127.0)
    codes = (blocks / scale).astype(np.float32).astype(dtype).astype(np.float64)
    return np.moveaxis((codes * scale).reshape(v.shape), -1, axis)


WIDE = False


def mx_kscale(k):
    if not WIDE:
        return np.ones(k)
    levels = np.array([10, -10, 5, -5, 0])
    if k % 512:
        return np.exp2(np.random.permutation(np.resize(levels, k // 32))).repeat(32)
    a = np.empty((k // 512, 16))
    for p in range(k // 512):
        a[p, :8] = np.random.permutation(np.resize(levels, 8))
        for g in range(8):
            far = levels[np.abs(levels - a[p, g]) >= 10]
            a[p, g + 8] = far[np.random.randint(len(far))]
    return np.exp2(a.ravel()).repeat(32)


def f64(x):
    return np.asarray(x).astype(np.float64)


def striped(idx):
    return np.tile(np.asarray(idx).reshape(-1, 16).T, (8, 1)).astype(np.uint16)


def unstriped(offs):
    return offs[:16].T.reshape(-1).astype(np.int64)


E2M1 = np.array([0.0, 0.5, 1.0, 1.5, 2.0, 3.0, 4.0, 6.0, -0.0, -0.5, -1.0, -1.5, -2.0, -3.0, -4.0, -6.0])


def pack_weight(w, fmt):
    k, n = w.shape
    w = f64(np.asarray(w, np.float32).astype(ml_dtypes.bfloat16)).reshape(k // 32, 32, n)
    amax = np.abs(w).max(1)
    if fmt == "e4m3":
        byte = np.frexp(amax)[1] - 1 + 127 - 7
    else:
        mant, ex = np.frexp(amax / 6.0)
        byte = np.where(mant > 0.5, ex, ex - 1) + 127
    byte = np.clip(np.where(amax > 0, byte, 1), 1, 254)
    scaled = (w * np.exp2(127.0 - byte)[:, None, :]).reshape(k, n).astype(np.float32)
    by_word = np.ascontiguousarray(scaled.reshape(k // 512, 128, 4, n).transpose(0, 1, 3, 2))
    if fmt == "e4m3":
        words = by_word.astype(ml_dtypes.float8_e4m3fn).view(np.uint8)
    else:
        c = by_word.astype(ml_dtypes.float4_e2m1fn).view(np.uint8) & 0xF
        words = (c[..., 0::2] | (c[..., 1::2] << 4)).reshape(k // 512, 128, 2 * n)
    return np.ascontiguousarray(words), np.ascontiguousarray(byte.astype(np.uint8).reshape(k // 512, 16, n))


def unpack_weight(words, scales, fmt):
    g, _, n = scales.shape
    words = np.ascontiguousarray(words).reshape(g, 128, n, -1)
    if fmt == "e4m3":
        vals = words.view(ml_dtypes.float8_e4m3fn).astype(np.float64)
    else:
        nib = np.empty((g, 128, n, 4), np.uint8)
        nib[..., 0::2] = words & 0xF
        nib[..., 1::2] = words >> 4
        vals = E2M1[nib]
    vals = vals * np.repeat(np.exp2(scales.astype(np.float64) - 127.0), 8, axis=1)[..., None]
    return vals.transpose(0, 1, 3, 2).reshape(g * 512, n)


D, E, T, I, G, U, Q = 512, 512, 4096, 1024, 64, 512, 128


def setup_inputs():
    n = np.random.standard_normal
    idx = np.random.permutation(T)[:I]
    idx2 = np.random.permutation(U)[:G]
    fd = mx_kscale(D)
    fe = mx_kscale(E)
    keysp = pack_weight(n((D, T)) / fd[:, None], "e4m3")
    valsp = pack_weight(n((E, T)) / fe[:, None], "e4m3")
    return {
        "query": (n((D, Q)) * 0.6 / np.sqrt(D) * fd[:, None]).astype(np.float32),
        "keys_words": keysp[0],
        "keys_scales": keysp[1],
        "ptab": (0.5 * n((Q, U)) - 0.4).astype(np.float32),
        "age": (np.random.uniform(0.0, 2.0, (1, I))).astype(np.float32),
        "gout": (n((E, Q)) * 1 / np.sqrt(E) * fe[:, None]).astype(np.float32),
        "vals_words": valsp[0],
        "vals_scales": valsp[1],
        "dquery": (n((D, Q)) * 1.0 / np.sqrt(D) * fd[:, None]).astype(np.float32),
        "base": (0.5 * n((Q, G))).astype(np.float32),
        "offs": striped(idx),
        "offs2": striped(idx2),
    }


def reference(query, keys_words, keys_scales, ptab, age, gout, vals_words, vals_scales, dquery, base, offs, offs2):
    idx = unstriped(offs)
    idx2 = unstriped(offs2)
    keysu = unpack_weight(keys_words, keys_scales, "e4m3")
    valsu = unpack_weight(vals_words, vals_scales, "e4m3")
    queryq = mxq(f64(query), 0, "e4m3")
    keysidxg = keysu[:, idx]
    a = queryq.T @ keysidxg
    dqueryq = mxq(f64(dquery), 0, "e4m3")
    ta = dqueryq.T @ keysidxg
    tp = np.exp(f64(ptab)[:, idx2])
    tr1 = np.repeat(tp, I // G, axis=1)
    p = np.exp(a - f64(age) * tr1)
    z = np.sum(p, axis=1, keepdims=True)
    goutq = mxq(f64(gout), 0, "e4m3")
    valsidxg = valsu[:, idx]
    c0 = goutq.T @ valsidxg
    dz = np.sum(p * c0, axis=1, keepdims=True) / np.square(z) * (-1.0)
    dp = 1.0 / z * c0 + dz
    xp = ta * p
    xz = np.sum(xp, axis=1, keepdims=True)
    xdz = (np.sum(xp * c0, axis=1, keepdims=True) - xz * z * 2.0 * np.sum(p * c0, axis=1, keepdims=True) / np.square(z)) / np.square(z) * (-1.0)
    xdp = xz * 1.0 / np.square(z) * (-1.0) * c0 + xdz
    xdtr1 = (xdp * p + xp * dp) * (-1.0) * f64(age)
    xdtp = xdtr1.reshape(Q, G, I // G).sum(axis=2)
    y = xdtp * 64.0 + f64(base)
    return y

@@ -1,0 +1,235 @@
+from contextlib import ExitStack
+import math
+
+import concourse.mybir as mybir
+from concourse.masks import make_identity
+
+F32 = mybir.dt.float32
+BF16 = mybir.dt.bfloat16
+I32 = mybir.dt.int32
+U32 = mybir.dt.uint32
+U16 = mybir.dt.uint16
+U8 = mybir.dt.uint8
+FP8X4 = mybir.dt.float8_e4m3fn_x4
+ALU = mybir.AluOpType
+ACT = mybir.ActivationFunctionType
+AXIS = mybir.AxisListType
+
+P = 128
+TOKENS = 4096
+SLOTS = 1024
+PAGES = 64
+TABLE = 512
+Q = 128
+HALVES = 2
+HALF = SLOTS // HALVES
+PACK = 4
+QUADS = HALF // PACK
+HALF_PAGES = PAGES // HALVES
+VAL_ROW = 4
+COOL = 8.0
+OUT_SCALE = 64.0
+
+FLOPS = 3 * 2 * 512 * Q * SLOTS
+
+
+def tile_attend_hvpagerate_kernel(tc, query, keys_words, keys_scales, ptab, age, gout, vals_words, vals_scales,
+                                   dquery, base, offs, offs2, out):
+    nc = tc.nc
+    with ExitStack() as ctx:
+        keep = ctx.enter_context(tc.tile_pool(name="keep", bufs=1))
+        psum = ctx.enter_context(tc.psum_pool(name="psum", bufs=1))
+
+        slot_list = keep.tile([P, SLOTS // 16], U16, name="slot_list")
+        page_list = keep.tile([P, PAGES // 16], U16, name="page_list")
+        nc.sync.dma_start(slot_list[:], offs)
+        nc.sync.dma_start(page_list[:], offs2)
+
+        key_plane = keep.tile([P, TOKENS], U8, name="key_plane", align_bytes=64)
+        val_plane = keep.tile([P, TOKENS], U8, name="val_plane", align_bytes=64)
+        nc.vector.memset(key_plane[:].bitcast(I32), 0)
+        nc.vector.memset(val_plane[:].bitcast(I32), 0)
+
+        def load_plane(queue, plane, scales, first_row):
+            for quad in range(4):
+                row = 32 * quad + first_row
+                queue.dma_start(plane[row:row + 4, :].bitcast(I32), scales[0, 4 * quad:4 * quad + 4, :].bitcast(I32))
+
+        def load_rows(queue, operand, name, tag):
+            raw = keep.tile([P, PACK, Q], F32, name=name, tag=tag, align_bytes=64)
+            queue.dma_start(raw[:], operand.rearrange("(p j) q -> p j q", j=PACK))
+            return raw
+
+        def load_words(words, name, tag):
+            pool_words = keep.tile([P, TOKENS], I32, name=name, tag=tag, align_bytes=64)
+            nc.scalar.dma_start(pool_words[:], words[0].rearrange("p n t -> p (n t)").bitcast(I32))
+            return pool_words
+
+        warm_in = keep.tile([P, 1], F32, name="warm_in", tag="gout_raw", align_bytes=64)
+        warm_out = keep.tile([P, 1], F32, name="warm_out", tag="key_words", align_bytes=64)
+        nc.vector.memset(warm_in[:], 0.0)
+        age_col = keep.tile([P, HALVES, PACK], F32, name="age_col")
+        nc.sync.dma_start(age_col[:], age[0].rearrange("(h n j) -> n h j", h=HALVES, j=PACK))
+        load_plane(nc.sync, key_plane, keys_scales, 0)
+        load_plane(nc.sync, val_plane, vals_scales, VAL_ROW)
+        query_raw = load_rows(nc.scalar, query, "query_raw", "query_raw")
+        dquery_raw = load_rows(nc.scalar, dquery, "dquery_raw", "val_words")
+        rate_table = keep.tile([P, TABLE], F32, name="rate_table")
+        nc.scalar.dma_start(rate_table[:], ptab)
+        nc.scalar.activation(warm_out[:], warm_in[:], ACT.Exp)
+        gout_raw = load_rows(nc.scalar, gout, "gout_raw", "gout_raw")
+        key_words = load_words(keys_words, "key_words", "key_words")
+
+        ident = keep.tile([P, P], F32, name="ident")
+        make_identity(nc, ident[:])
+        base_sb = keep.tile([P, PAGES], F32, name="base_sb")
+        nc.gpsimd.dma_start(base_sb[:], base)
+
+        def gather(window, dtype, name, first, count, tag):
+            got = keep.tile([P, count], dtype, name=name, tag=tag, align_bytes=64)
+            nc.vector.tensor_copy(got[:], window.indirect(slot_list[:, first // 16:(first + count) // 16]))
+            return got
+
+        key_scale = gather(key_plane[:], U8, "key_scale", 0, SLOTS, "key_scale")
+        val_scale = gather(val_plane[:], U8, "val_scale", 0, SLOTS, "val_scale")
+
+        qd_bf = keep.tile([P, 2 * Q, PACK], BF16, name="qd_bf", align_bytes=64)
+        nc.scalar.copy(qd_bf[:, 0:Q, :], query_raw[:].rearrange("p j q -> p q j"))
+        nc.scalar.copy(qd_bf[:, Q:2 * Q, :], dquery_raw[:].rearrange("p j q -> p q j"))
+        qd_codes = keep.tile([P, 2 * Q], U32, name="qd_codes", align_bytes=64)
+        qd_scale = keep.tile([P, 2 * Q], U8, name="qd_scale", align_bytes=64)
+        nc.vector.quantize_mx(out=qd_codes[:].bitcast(FP8X4), scales=qd_scale[:],
+                              in_=qd_bf[:].rearrange("p q j -> p (q j)"))
+
+        val_words = load_words(vals_words, "val_words", "val_words")
+        gout_bf = keep.tile([P, Q, PACK], BF16, name="gout_bf", align_bytes=64)
+        nc.scalar.copy(gout_bf[:], gout_raw[:].rearrange("p j q -> p q j"))
+        gout_codes = keep.tile([P, Q], U32, name="gout_codes", align_bytes=64)
+        gout_scale = keep.tile([P, Q], U8, name="gout_scale", align_bytes=64)
+        nc.vector.quantize_mx(out=gout_codes[:].bitcast(FP8X4), scales=gout_scale[:],
+                              in_=gout_bf[:].rearrange("p q j -> p (q j)"))
+
+        log_rate = keep.tile([P, PAGES], F32, name="log_rate")
+        nc.vector.tensor_copy(log_rate[:], rate_table[:].indirect(page_list[:]))
+        rate = keep.tile([P, PAGES], F32, name="rate")
+        nc.scalar.activation(rate[:], log_rate[:], ACT.Exp)
+        fade = []
+        for h in range(HALVES):
+            age_row = psum.tile([P, PACK, QUADS], F32, name=f"age_row{h}", tag="turn", bufs=2)
+            for j in range(PACK):
+                nc.tensor.transpose(age_row[:, j, :], age_col[:, h, j:j + 1].to_broadcast([P, P]), ident[:])
+            fade_h = keep.tile([P, PACK, QUADS], F32, name=f"fade{h}", tag=f"fade{h}", align_bytes=64)
+            rate_h = rate[:, h * HALF_PAGES:(h + 1) * HALF_PAGES]
+            nc.vector.tensor_tensor(
+                fade_h[:].rearrange("p j (g r) -> p j g r", r=PACK),
+                age_row[:].rearrange("p j (g r) -> p j g r", r=PACK),
+                rate_h.unsqueeze(1).unsqueeze(3).to_broadcast([P, PACK, HALF_PAGES, PACK]),
+                ALU.mult)
+            fade.append(fade_h)
+
+        def product(name, tag, codes, scale, words, words_scale):
+            bank = psum.tile([P, HALF], F32, name=name, tag=tag)
+            nc.tensor.matmul_mx(out=bank[:], lhsT=codes.bitcast(FP8X4), lhsT_scale=scale,
+                                rhs=words[:].bitcast(FP8X4), rhs_scale=words_scale, start=True, stop=True)
+            return bank[:].rearrange("p (n j) -> p j n", j=PACK)
+
+        score, tangent = [], []
+        for h in range(HALVES):
+            keys_h = gather(key_words[:].bitcast(U32), U32, f"keys{h}", h * HALF, HALF, f"keys{h}")
+            cols = slice(h * HALF, (h + 1) * HALF)
+            score.append(product(f"score{h}", f"score{h}", qd_codes[:, 0:Q], qd_scale[:, 0:Q], keys_h, key_scale[:, cols]))
+            tangent.append(product(f"tangent{h}", f"tangent{h}", qd_codes[:, Q:2 * Q], qd_scale[:, Q:2 * Q], keys_h,
+                                   key_scale[:, cols]))
+
+        def slots_tile(name):
+            return keep.tile([P, PACK, QUADS], F32, name=name)
+
+        def column(name):
+            return keep.tile([P, 1], F32, name=name)
+
+        logit = [slots_tile(f"logit{h}") for h in range(HALVES)]
+        weight = [slots_tile(f"weight{h}") for h in range(HALVES)]
+        cool_sum = [column(f"cool_sum{h}") for h in range(HALVES)]
+        for h in range(HALVES):
+            nc.vector.tensor_tensor(logit[h][:], score[h], fade[h][:], ALU.subtract)
+            nc.scalar.activation(weight[h][:], logit[h][:], ACT.Exp, scale=1.0 / COOL, accum_out=cool_sum[h][:])
+
+        cool_total = column("cool_total")
+        nc.scalar.activation(cool_total[:], cool_sum[0][:], ACT.Identity, bias=cool_sum[1][:])
+        shift = column("shift")
+        nc.scalar.activation(shift[:], cool_total[:].bitcast(U32), ACT.Copy,
+                             scale=-COOL * math.log(2.0) / 2.0 ** 23,
+                             bias=COOL * (127.0 * math.log(2.0) + 0.5 * math.log(SLOTS)))
+        norm_part = [column(f"norm_part{h}") for h in range(HALVES)]
+        for h in range(HALVES):
+            nc.scalar.activation(weight[h][:], logit[h][:], ACT.Exp, bias=shift[:], accum_out=norm_part[h][:])
+        norm = column("norm")
+        nc.scalar.activation(norm[:], norm_part[0][:], ACT.Identity, bias=norm_part[1][:])
+
+        def aged_quad_sums(values, h, sums, name):
+            turned = psum.tile([P, PACK, Q], F32, name=name + "_turned", tag="turn", bufs=2)
+            for j in range(PACK):
+                nc.tensor.transpose(turned[:, j, :], values[:, j, :], ident[:])
+            aged = keep.tile([P, PACK, Q], F32, name=name + "_aged")
+            for j in range(PACK):
+                nc.scalar.activation(aged[:, j, :], turned[:, j, :], ACT.Copy, scale=age_col[:, h, j:j + 1])
+            for j in range(PACK):
+                nc.tensor.matmul(sums, lhsT=aged[:, j, :], rhs=ident[:], is_transpose=True,
+                                 start=(j == 0), stop=(j == PACK - 1))
+
+        centred = [slots_tile(f"centred{h}") for h in range(HALVES)]
+        tangent_part = [column(f"tangent_part{h}") for h in range(HALVES)]
+        for h in range(HALVES):
+            nc.vector.scalar_tensor_tensor(centred[h][:], weight[h][:], 1.0, tangent[h], ALU.mult, ALU.mult,
+                                           accum_out=tangent_part[h][:])
+        inv_norm = column("inv_norm")
+        nc.vector.reciprocal(inv_norm[:], norm[:])
+        tangent_mean = column("tangent_mean")
+        nc.vector.tensor_scalar(tangent_mean[:], tangent_part[0][:], tangent_part[1][:], inv_norm[:], ALU.add, ALU.mult)
+        out_factor = column("out_factor")
+        nc.vector.tensor_scalar(out_factor[:], inv_norm[:], -OUT_SCALE, None, ALU.mult)
+        mean_factor = column("mean_factor")
+        nc.vector.tensor_scalar(mean_factor[:], inv_norm[:], -OUT_SCALE, inv_norm[:], ALU.mult, ALU.mult)
+
+        early_sums = psum.tile([P, 2, HALVES, QUADS], F32, name="early_sums", tag="score0")
+        for h in range(HALVES):
+            aged_quad_sums(weight[h], h, early_sums[:, 0, h, :], f"weight{h}")
+        for h in range(HALVES):
+            nc.vector.scalar_tensor_tensor(centred[h][:], tangent[h], tangent_mean[:], weight[h][:],
+                                           ALU.subtract, ALU.mult)
+            aged_quad_sums(centred[h], h, early_sums[:, 1, h, :], f"centred{h}")
+
+        pull = []
+        for h in range(HALVES):
+            vals_h = gather(val_words[:].bitcast(U32), U32, f"vals{h}", h * HALF, HALF, f"fade{1 - h}")
+            pull.append(product(f"pull{h}", f"pull{h}", gout_codes[:], gout_scale[:], vals_h,
+                                val_scale[VAL_ROW:P, h * HALF:(h + 1) * HALF]))
+
+        early_pages = keep.tile([P, 2, PAGES], F32, name="early_pages")
+        nc.vector.tensor_reduce(early_pages[:].rearrange("p s g -> p (s g)"),
+                                early_sums[:].rearrange("p s h (g r) -> p (s h g) r", r=PACK), AXIS.X, ALU.add)
+
+        late_sums = psum.tile([P, HALVES, QUADS], F32, name="late_sums", tag="score1")
+        cross = [slots_tile(f"cross{h}") for h in range(HALVES)]
+        cov_part = [column(f"cov_part{h}") for h in range(HALVES)]
+        mean_part = [column(f"mean_part{h}") for h in range(HALVES)]
+        for h in range(HALVES):
+            nc.vector.scalar_tensor_tensor(cross[h][:], centred[h][:], out_factor[:], pull[h], ALU.mult, ALU.mult,
+                                           accum_out=cov_part[h][:])
+            aged_quad_sums(cross[h], h, late_sums[:, h, :], f"cross{h}")
+        cov_factor = column("cov_factor")
+        nc.vector.tensor_scalar(cov_factor[:], cov_part[0][:], cov_part[1][:], inv_norm[:], ALU.add, ALU.mult)
+        rest = keep.tile([P, PAGES], F32, name="rest")
+        nc.vector.scalar_tensor_tensor(rest[:], early_pages[:, 0, :], cov_factor[:], base_sb[:], ALU.mult, ALU.subtract)
+        for h in range(HALVES):
+            nc.vector.scalar_tensor_tensor(logit[h][:], weight[h][:], mean_factor[:], pull[h], ALU.mult, ALU.mult,
+                                           accum_out=mean_part[h][:])
+            rest_next = keep.tile([P, PAGES], F32, name=f"rest{h}")
+            nc.vector.scalar_tensor_tensor(rest_next[:], early_pages[:, 1, :], mean_part[h][:], rest[:], ALU.mult, ALU.add)
+            rest = rest_next
+
+        late_pages = keep.tile([P, PAGES], F32, name="late_pages")
+        nc.vector.tensor_reduce(late_pages[:], late_sums[:].rearrange("p h (g r) -> p (h g) r", r=PACK), AXIS.X, ALU.add)
+        result = keep.tile([P, PAGES], F32, name="result")
+        nc.vector.tensor_tensor(result[:], late_pages[:], rest[:], ALU.subtract)
+        nc.sync.dma_start(out, result[:])

@@ -2,7 +2,6 @@ from contextlib import ExitStack
 import math
 
 import concourse.mybir as mybir
-from concourse.masks import make_identity
 
 F32 = mybir.dt.float32
 BF16 = mybir.dt.bfloat16
@@ -48,7 +47,6 @@ def tile_attend_hvpagerate_kernel(tc, query, keys_words, keys_scales, ptab, age,
         key_plane = keep.tile([P, TOKENS], U8, name="key_plane", align_bytes=64)
         val_plane = keep.tile([P, TOKENS], U8, name="val_plane", align_bytes=64)
         nc.vector.memset(key_plane[:].bitcast(I32), 0)
-        nc.vector.memset(val_plane[:].bitcast(I32), 0)
 
         def load_plane(queue, plane, scales, first_row):
             for quad in range(4):
@@ -62,28 +60,24 @@ def tile_attend_hvpagerate_kernel(tc, query, keys_words, keys_scales, ptab, age,
 
         def load_words(words, name, tag):
             pool_words = keep.tile([P, TOKENS], I32, name=name, tag=tag, align_bytes=64)
-            nc.scalar.dma_start(pool_words[:], words[0].rearrange("p n t -> p (n t)").bitcast(I32))
+            nc.sync.dma_start(pool_words[:], words[0].rearrange("p n t -> p (n t)").bitcast(I32))
             return pool_words
 
-        warm_in = keep.tile([P, 1], F32, name="warm_in", tag="gout_raw", align_bytes=64)
-        warm_out = keep.tile([P, 1], F32, name="warm_out", tag="key_words", align_bytes=64)
-        nc.vector.memset(warm_in[:], 0.0)
         age_col = keep.tile([P, HALVES, PACK], F32, name="age_col")
         nc.sync.dma_start(age_col[:], age[0].rearrange("(h n j) -> n h j", h=HALVES, j=PACK))
         load_plane(nc.sync, key_plane, keys_scales, 0)
-        load_plane(nc.sync, val_plane, vals_scales, VAL_ROW)
-        query_raw = load_rows(nc.scalar, query, "query_raw", "query_raw")
+        query_raw = load_rows(nc.scalar, query, "query_raw", "gout_raw")
         dquery_raw = load_rows(nc.scalar, dquery, "dquery_raw", "val_words")
-        rate_table = keep.tile([P, TABLE], F32, name="rate_table")
-        nc.scalar.dma_start(rate_table[:], ptab)
-        nc.scalar.activation(warm_out[:], warm_in[:], ACT.Exp)
-        gout_raw = load_rows(nc.scalar, gout, "gout_raw", "gout_raw")
-        key_words = load_words(keys_words, "key_words", "key_words")
-
+        rate_table = keep.tile([P, TABLE], F32, name="rate_table", tag="base_sb")
+        nc.gpsimd.dma_start(rate_table[:], ptab)
+        ones = keep.tile([P, P], F32, name="ones", tag="key_words", align_bytes=64)
+        nc.gpsimd.memset(ones[:], 1.0)
         ident = keep.tile([P, P], F32, name="ident")
-        make_identity(nc, ident[:])
-        base_sb = keep.tile([P, PAGES], F32, name="base_sb")
-        nc.gpsimd.dma_start(base_sb[:], base)
+        nc.gpsimd.affine_select(out=ident[:], in_=ones[:], compare_op=ALU.is_equal, fill=0.0, base=0,
+                                pattern=[[-1, P]], channel_multiplier=1)
+        key_words = load_words(keys_words, "key_words", "key_words")
+        nc.gpsimd.memset(val_plane[:].bitcast(I32), 0)
+        load_plane(nc.sync, val_plane, vals_scales, VAL_ROW)
 
         def gather(window, dtype, name, first, count, tag):
             got = keep.tile([P, count], dtype, name=name, tag=tag, align_bytes=64)
@@ -91,10 +85,10 @@ def tile_attend_hvpagerate_kernel(tc, query, keys_words, keys_scales, ptab, age,
             return got
 
         key_scale = gather(key_plane[:], U8, "key_scale", 0, SLOTS, "key_scale")
-        val_scale = gather(val_plane[:], U8, "val_scale", 0, SLOTS, "val_scale")
 
         qd_bf = keep.tile([P, 2 * Q, PACK], BF16, name="qd_bf", align_bytes=64)
         nc.scalar.copy(qd_bf[:, 0:Q, :], query_raw[:].rearrange("p j q -> p q j"))
+        gout_raw = load_rows(nc.sync, gout, "gout_raw", "gout_raw")
         nc.scalar.copy(qd_bf[:, Q:2 * Q, :], dquery_raw[:].rearrange("p j q -> p q j"))
         qd_codes = keep.tile([P, 2 * Q], U32, name="qd_codes", align_bytes=64)
         qd_scale = keep.tile([P, 2 * Q], U8, name="qd_scale", align_bytes=64)
@@ -102,30 +96,32 @@ def tile_attend_hvpagerate_kernel(tc, query, keys_words, keys_scales, ptab, age,
                               in_=qd_bf[:].rearrange("p q j -> p (q j)"))
 
         val_words = load_words(vals_words, "val_words", "val_words")
-        gout_bf = keep.tile([P, Q, PACK], BF16, name="gout_bf", align_bytes=64)
-        nc.scalar.copy(gout_bf[:], gout_raw[:].rearrange("p j q -> p q j"))
-        gout_codes = keep.tile([P, Q], U32, name="gout_codes", align_bytes=64)
-        gout_scale = keep.tile([P, Q], U8, name="gout_scale", align_bytes=64)
-        nc.vector.quantize_mx(out=gout_codes[:].bitcast(FP8X4), scales=gout_scale[:],
-                              in_=gout_bf[:].rearrange("p q j -> p (q j)"))
-
         log_rate = keep.tile([P, PAGES], F32, name="log_rate")
         nc.vector.tensor_copy(log_rate[:], rate_table[:].indirect(page_list[:]))
-        rate = keep.tile([P, PAGES], F32, name="rate")
-        nc.scalar.activation(rate[:], log_rate[:], ACT.Exp)
+        rate = keep.tile([P, PAGES, PACK], F32, name="rate")
+        nc.scalar.activation(rate[:], log_rate[:].unsqueeze(2).to_broadcast([P, PAGES, PACK]), ACT.Exp)
+        base_sb = keep.tile([P, PAGES], F32, name="base_sb", tag="base_sb")
+        nc.sync.dma_start(base_sb[:], base)
+        rate_turned = psum.tile([P, HALVES, Q], F32, name="rate_turned", tag="pull0")
+        rate_quads = rate[:].rearrange("p g r -> p (g r)")
+        for h in range(HALVES):
+            nc.tensor.transpose(rate_turned[:, h, :], rate_quads[:, h * QUADS:(h + 1) * QUADS], ident[:])
         fade = []
         for h in range(HALVES):
-            age_row = psum.tile([P, PACK, QUADS], F32, name=f"age_row{h}", tag="turn", bufs=2)
+            fade_turned = keep.tile([P, PACK, Q], F32, name=f"fade_turned{h}", tag=f"fade_turned{h}", align_bytes=64)
+            fade_bank = psum.tile([P, PACK, QUADS], F32, name=f"fade_bank{h}", tag="turn", bufs=2)
             for j in range(PACK):
-                nc.tensor.transpose(age_row[:, j, :], age_col[:, h, j:j + 1].to_broadcast([P, P]), ident[:])
+                nc.scalar.activation(fade_turned[:, j, :], rate_turned[:, h, :], ACT.Copy, scale=age_col[:, h, j:j + 1])
+                nc.tensor.transpose(fade_bank[:, j, :], fade_turned[:, j, :], ident[:])
             fade_h = keep.tile([P, PACK, QUADS], F32, name=f"fade{h}", tag=f"fade{h}", align_bytes=64)
-            rate_h = rate[:, h * HALF_PAGES:(h + 1) * HALF_PAGES]
-            nc.vector.tensor_tensor(
-                fade_h[:].rearrange("p j (g r) -> p j g r", r=PACK),
-                age_row[:].rearrange("p j (g r) -> p j g r", r=PACK),
-                rate_h.unsqueeze(1).unsqueeze(3).to_broadcast([P, PACK, HALF_PAGES, PACK]),
-                ALU.mult)
+            nc.scalar.copy(fade_h[:], fade_bank[:])
             fade.append(fade_h)
+
+        age_bank = psum.tile([P, PACK, QUADS], F32, name="age_bank", tag="pull1")
+        for j in range(PACK):
+            nc.tensor.transpose(age_bank[:, j, :], age_col[:, 1, j:j + 1].to_broadcast([P, P]), ident[:])
+        age_row = keep.tile([P, PACK, QUADS], F32, name="age_row")
+        nc.scalar.copy(age_row[:], age_bank[:])
 
         def product(name, tag, codes, scale, words, words_scale):
             bank = psum.tile([P, HALF], F32, name=name, tag=tag)
@@ -154,9 +150,18 @@ def tile_attend_hvpagerate_kernel(tc, query, keys_words, keys_scales, ptab, age,
             nc.vector.tensor_tensor(logit[h][:], score[h], fade[h][:], ALU.subtract)
             nc.scalar.activation(weight[h][:], logit[h][:], ACT.Exp, scale=1.0 / COOL, accum_out=cool_sum[h][:])
 
-        cool_total = column("cool_total")
+        gout_bf = keep.tile([P, Q, PACK], BF16, name="gout_bf", tag="fade_turned1", align_bytes=64)
+        nc.scalar.copy(gout_bf[:], gout_raw[:].rearrange("p j q -> p q j"))
+        gout_codes = keep.tile([P, Q], U32, name="gout_codes", tag="keys0", align_bytes=64)
+        gout_scale = keep.tile([P, Q], U8, name="gout_scale", align_bytes=64)
+        nc.vector.quantize_mx(out=gout_codes[:].bitcast(FP8X4), scales=gout_scale[:],
+                              in_=gout_bf[:].rearrange("p q j -> p (q j)"))
+
+        val_scale = gather(val_plane[:], U8, "val_scale", 0, SLOTS, "fade1")
+
+        cool_total = keep.tile([P, 1], F32, name="cool_total", tag="vals0", align_bytes=64)
         nc.scalar.activation(cool_total[:], cool_sum[0][:], ACT.Identity, bias=cool_sum[1][:])
-        shift = column("shift")
+        shift = keep.tile([P, 1], F32, name="shift", tag="vals1", align_bytes=64)
         nc.scalar.activation(shift[:], cool_total[:].bitcast(U32), ACT.Copy,
                              scale=-COOL * math.log(2.0) / 2.0 ** 23,
                              bias=COOL * (127.0 * math.log(2.0) + 0.5 * math.log(SLOTS)))
@@ -177,59 +182,58 @@ def tile_attend_hvpagerate_kernel(tc, query, keys_words, keys_scales, ptab, age,
                 nc.tensor.matmul(sums, lhsT=aged[:, j, :], rhs=ident[:], is_transpose=True,
                                  start=(j == 0), stop=(j == PACK - 1))
 
-        centred = [slots_tile(f"centred{h}") for h in range(HALVES)]
-        tangent_part = [column(f"tangent_part{h}") for h in range(HALVES)]
-        for h in range(HALVES):
-            nc.vector.scalar_tensor_tensor(centred[h][:], weight[h][:], 1.0, tangent[h], ALU.mult, ALU.mult,
-                                           accum_out=tangent_part[h][:])
-        inv_norm = column("inv_norm")
-        nc.vector.reciprocal(inv_norm[:], norm[:])
-        tangent_mean = column("tangent_mean")
-        nc.vector.tensor_scalar(tangent_mean[:], tangent_part[0][:], tangent_part[1][:], inv_norm[:], ALU.add, ALU.mult)
-        out_factor = column("out_factor")
-        nc.vector.tensor_scalar(out_factor[:], inv_norm[:], -OUT_SCALE, None, ALU.mult)
-        mean_factor = column("mean_factor")
-        nc.vector.tensor_scalar(mean_factor[:], inv_norm[:], -OUT_SCALE, inv_norm[:], ALU.mult, ALU.mult)
-
-        early_sums = psum.tile([P, 2, HALVES, QUADS], F32, name="early_sums", tag="score0")
-        for h in range(HALVES):
-            aged_quad_sums(weight[h], h, early_sums[:, 0, h, :], f"weight{h}")
-        for h in range(HALVES):
-            nc.vector.scalar_tensor_tensor(centred[h][:], tangent[h], tangent_mean[:], weight[h][:],
-                                           ALU.subtract, ALU.mult)
-            aged_quad_sums(centred[h], h, early_sums[:, 1, h, :], f"centred{h}")
-
         pull = []
         for h in range(HALVES):
-            vals_h = gather(val_words[:].bitcast(U32), U32, f"vals{h}", h * HALF, HALF, f"fade{1 - h}")
+            vals_h = gather(val_words[:].bitcast(U32), U32, f"vals{h}", h * HALF, HALF, f"vals{h}")
             pull.append(product(f"pull{h}", f"pull{h}", gout_codes[:], gout_scale[:], vals_h,
                                 val_scale[VAL_ROW:P, h * HALF:(h + 1) * HALF]))
 
-        early_pages = keep.tile([P, 2, PAGES], F32, name="early_pages")
-        nc.vector.tensor_reduce(early_pages[:].rearrange("p s g -> p (s g)"),
-                                early_sums[:].rearrange("p s h (g r) -> p (s h g) r", r=PACK), AXIS.X, ALU.add)
+        early_sums = psum.tile([P, HALVES, QUADS], F32, name="early_sums", tag="score0")
+        for h in range(HALVES):
+            aged_quad_sums(weight[h], h, early_sums[:, h, :], f"weight{h}")
 
-        late_sums = psum.tile([P, HALVES, QUADS], F32, name="late_sums", tag="score1")
         cross = [slots_tile(f"cross{h}") for h in range(HALVES)]
+        tangent_part = [column(f"tangent_part{h}") for h in range(HALVES)]
+        pull_part = [column(f"pull_part{h}") for h in range(HALVES)]
         cov_part = [column(f"cov_part{h}") for h in range(HALVES)]
-        mean_part = [column(f"mean_part{h}") for h in range(HALVES)]
         for h in range(HALVES):
-            nc.vector.scalar_tensor_tensor(cross[h][:], centred[h][:], out_factor[:], pull[h], ALU.mult, ALU.mult,
-                                           accum_out=cov_part[h][:])
-            aged_quad_sums(cross[h], h, late_sums[:, h, :], f"cross{h}")
-        cov_factor = column("cov_factor")
-        nc.vector.tensor_scalar(cov_factor[:], cov_part[0][:], cov_part[1][:], inv_norm[:], ALU.add, ALU.mult)
-        rest = keep.tile([P, PAGES], F32, name="rest")
-        nc.vector.scalar_tensor_tensor(rest[:], early_pages[:, 0, :], cov_factor[:], base_sb[:], ALU.mult, ALU.subtract)
+            nc.vector.scalar_tensor_tensor(logit[h][:], weight[h][:], 1.0, tangent[h], ALU.mult, ALU.mult,
+                                           accum_out=tangent_part[h][:])
+        inv_norm = column("inv_norm")
+        nc.vector.reciprocal(inv_norm[:], norm[:])
         for h in range(HALVES):
-            nc.vector.scalar_tensor_tensor(logit[h][:], weight[h][:], mean_factor[:], pull[h], ALU.mult, ALU.mult,
-                                           accum_out=mean_part[h][:])
-            rest_next = keep.tile([P, PAGES], F32, name=f"rest{h}")
-            nc.vector.scalar_tensor_tensor(rest_next[:], early_pages[:, 1, :], mean_part[h][:], rest[:], ALU.mult, ALU.add)
-            rest = rest_next
+            nc.vector.scalar_tensor_tensor(cross[h][:], weight[h][:], 1.0, pull[h], ALU.mult, ALU.mult,
+                                           accum_out=pull_part[h][:])
+        tangent_mean = column("tangent_mean")
+        nc.vector.tensor_scalar(tangent_mean[:], tangent_part[0][:], tangent_part[1][:], inv_norm[:], ALU.add, ALU.mult)
+        pull_mean = column("pull_mean")
+        nc.vector.tensor_scalar(pull_mean[:], pull_part[0][:], pull_part[1][:], inv_norm[:], ALU.add, ALU.mult)
+        out_factor = column("out_factor")
+        nc.scalar.activation(out_factor[:], inv_norm[:], ACT.Copy, scale=-OUT_SCALE)
 
+        late_sums = psum.tile([P, QUADS], F32, name="late_sums", tag="score1")
         late_pages = keep.tile([P, PAGES], F32, name="late_pages")
-        nc.vector.tensor_reduce(late_pages[:], late_sums[:].rearrange("p h (g r) -> p (h g) r", r=PACK), AXIS.X, ALU.add)
+        for h in range(HALVES):
+            centred = keep.tile([P, PACK, QUADS], F32, name=f"centred{h}", tag="centred")
+            nc.vector.scalar_tensor_tensor(centred[:], tangent[h], tangent_mean[:], weight[h][:],
+                                           ALU.subtract, ALU.mult)
+            nc.vector.scalar_tensor_tensor(cross[h][:], pull[h], pull_mean[:], centred[:], ALU.subtract, ALU.mult,
+                                           accum_out=cov_part[h][:])
+        aged_quad_sums(cross[0], 0, late_sums[:], "cross0")
+        nc.vector.tensor_tensor(logit[1][:], cross[1][:], age_row[:], ALU.mult)
+        nc.vector.tensor_reduce(late_pages[:, HALF_PAGES:PAGES], logit[1][:].rearrange("p j (g r) -> p g j r", r=PACK),
+                                AXIS.XY, ALU.add)
+
+        early_pages = keep.tile([P, PAGES], F32, name="early_pages")
+        nc.vector.tensor_reduce(early_pages[:], early_sums[:].rearrange("p h (g r) -> p (h g) r", r=PACK), AXIS.X, ALU.add)
+        covariance = column("covariance")
+        nc.vector.tensor_scalar(covariance[:], cov_part[0][:], cov_part[1][:], inv_norm[:], ALU.add, ALU.mult)
+        spread = keep.tile([P, PAGES], F32, name="spread")
+        nc.vector.tensor_scalar(spread[:], early_pages[:], covariance[:], out_factor[:], ALU.mult, ALU.mult)
+        rest = keep.tile([P, PAGES], F32, name="rest")
+        nc.vector.tensor_tensor(rest[:], base_sb[:], spread[:], ALU.subtract)
+
+        nc.vector.tensor_reduce(late_pages[:, 0:HALF_PAGES], late_sums[:].rearrange("p (g r) -> p g r", r=PACK), AXIS.X, ALU.add)
         result = keep.tile([P, PAGES], F32, name="result")
-        nc.vector.tensor_tensor(result[:], late_pages[:], rest[:], ALU.subtract)
+        nc.vector.scalar_tensor_tensor(result[:], late_pages[:], out_factor[:], rest[:], ALU.mult, ALU.add)
         nc.sync.dma_start(out, result[:])

@@ -113,21 +113,21 @@ def tile_attend_hvpagerate_kernel(tc, query, keys_words, keys_scales, ptab, age,
             for j in range(PACK):
                 nc.scalar.activation(fade_turned[:, j, :], rate_turned[:, h, :], ACT.Copy, scale=age_col[:, h, j:j + 1])
                 nc.tensor.transpose(fade_bank[:, j, :], fade_turned[:, j, :], ident[:])
-            fade_h = keep.tile([P, PACK, QUADS], F32, name=f"fade{h}", tag=f"fade{h}", align_bytes=64)
-            nc.scalar.copy(fade_h[:], fade_bank[:])
+            fade_h = keep.tile([P, HALF], F32, name=f"fade{h}", tag=f"fade{h}", align_bytes=64)
+            nc.scalar.copy(fade_h[:].rearrange("p (n j) -> p n j", j=PACK), fade_bank[:].rearrange("p j n -> p n j"))
             fade.append(fade_h)
 
         age_bank = psum.tile([P, PACK, QUADS], F32, name="age_bank", tag="pull1")
         for j in range(PACK):
             nc.tensor.transpose(age_bank[:, j, :], age_col[:, 1, j:j + 1].to_broadcast([P, P]), ident[:])
-        age_row = keep.tile([P, PACK, QUADS], F32, name="age_row")
-        nc.scalar.copy(age_row[:], age_bank[:])
+        age_row = keep.tile([P, HALF], F32, name="age_row")
+        nc.scalar.copy(age_row[:].rearrange("p (n j) -> p n j", j=PACK), age_bank[:].rearrange("p j n -> p n j"))
 
         def product(name, tag, codes, scale, words, words_scale):
             bank = psum.tile([P, HALF], F32, name=name, tag=tag)
             nc.tensor.matmul_mx(out=bank[:], lhsT=codes.bitcast(FP8X4), lhsT_scale=scale,
                                 rhs=words[:].bitcast(FP8X4), rhs_scale=words_scale, start=True, stop=True)
-            return bank[:].rearrange("p (n j) -> p j n", j=PACK)
+            return bank[:]
 
         score, tangent = [], []
         for h in range(HALVES):
@@ -138,7 +138,7 @@ def tile_attend_hvpagerate_kernel(tc, query, keys_words, keys_scales, ptab, age,
                                    key_scale[:, cols]))
 
         def slots_tile(name):
-            return keep.tile([P, PACK, QUADS], F32, name=name)
+            return keep.tile([P, HALF], F32, name=name)
 
         def column(name):
             return keep.tile([P, 1], F32, name=name)
@@ -174,7 +174,7 @@ def tile_attend_hvpagerate_kernel(tc, query, keys_words, keys_scales, ptab, age,
         def aged_quad_sums(values, h, sums, name):
             turned = psum.tile([P, PACK, Q], F32, name=name + "_turned", tag="turn", bufs=2)
             for j in range(PACK):
-                nc.tensor.transpose(turned[:, j, :], values[:, j, :], ident[:])
+                nc.tensor.transpose(turned[:, j, :], values[:].rearrange("p (n j) -> p j n", j=PACK)[:, j, :], ident[:])
             aged = keep.tile([P, PACK, Q], F32, name=name + "_aged")
             for j in range(PACK):
                 nc.scalar.activation(aged[:, j, :], turned[:, j, :], ACT.Copy, scale=age_col[:, h, j:j + 1])
@@ -214,15 +214,15 @@ def tile_attend_hvpagerate_kernel(tc, query, keys_words, keys_scales, ptab, age,
         late_sums = psum.tile([P, QUADS], F32, name="late_sums", tag="score1")
         late_pages = keep.tile([P, PAGES], F32, name="late_pages")
         for h in range(HALVES):
-            centred = keep.tile([P, PACK, QUADS], F32, name=f"centred{h}", tag="centred")
+            centred = keep.tile([P, HALF], F32, name=f"centred{h}", tag="centred")
             nc.vector.scalar_tensor_tensor(centred[:], tangent[h], tangent_mean[:], weight[h][:],
                                            ALU.subtract, ALU.mult)
             nc.vector.scalar_tensor_tensor(cross[h][:], pull[h], pull_mean[:], centred[:], ALU.subtract, ALU.mult,
                                            accum_out=cov_part[h][:])
         aged_quad_sums(cross[0], 0, late_sums[:], "cross0")
         nc.vector.tensor_tensor(logit[1][:], cross[1][:], age_row[:], ALU.mult)
-        nc.vector.tensor_reduce(late_pages[:, HALF_PAGES:PAGES], logit[1][:].rearrange("p j (g r) -> p g j r", r=PACK),
-                                AXIS.XY, ALU.add)
+        nc.vector.tensor_reduce(late_pages[:, HALF_PAGES:PAGES], logit[1][:].rearrange("p (g s) -> p g s", s=16),
+                                AXIS.X, ALU.add)
 
         early_pages = keep.tile([P, PAGES], F32, name="early_pages")
         nc.vector.tensor_reduce(early_pages[:], early_sums[:].rearrange("p h (g r) -> p (h g) r", r=PACK), AXIS.X, ALU.add)

@@ -1,5 +1,5 @@
-from contextlib import ExitStack
 import math
+from contextlib import ExitStack
 
 import concourse.mybir as mybir
 
@@ -15,21 +15,30 @@ ACT = mybir.ActivationFunctionType
 AXIS = mybir.AxisListType
 
 P = 128
+Q = 128
+FEATURES = 512
+PACK = 4
 TOKENS = 4096
+TABLE = 512
 SLOTS = 1024
 PAGES = 64
-TABLE = 512
-Q = 128
+PAGE = SLOTS // PAGES
+LIST_COLUMN = 16
 HALVES = 2
 HALF = SLOTS // HALVES
-PACK = 4
-QUADS = HALF // PACK
 HALF_PAGES = PAGES // HALVES
-VAL_ROW = 4
+QUAD = 4
+QUADS = HALF // QUAD
+PAGE_QUADS = PAGE // QUAD
+SCALE_ROWS = 16
+QUADRANT = 32
+QUADRANT_ROWS = 4
+SPREAD = P // SCALE_ROWS
+MX_ALIGN = 64
 COOL = 8.0
 OUT_SCALE = 64.0
 
-FLOPS = 3 * 2 * 512 * Q * SLOTS
+FLOPS = 3 * 2 * FEATURES * Q * SLOTS
 
 
 def tile_attend_hvpagerate_kernel(tc, query, keys_words, keys_scales, ptab, age, gout, vals_words, vals_scales,
@@ -39,130 +48,147 @@ def tile_attend_hvpagerate_kernel(tc, query, keys_words, keys_scales, ptab, age,
         keep = ctx.enter_context(tc.tile_pool(name="keep", bufs=1))
         psum = ctx.enter_context(tc.psum_pool(name="psum", bufs=1))
 
-        slot_list = keep.tile([P, SLOTS // 16], U16, name="slot_list")
-        page_list = keep.tile([P, PAGES // 16], U16, name="page_list")
-        nc.sync.dma_start(slot_list[:], offs)
-        nc.sync.dma_start(page_list[:], offs2)
+        def shared(shape, dtype, name, tag):
+            return keep.tile(shape, dtype, name=name, tag=tag, align_bytes=MX_ALIGN)
 
-        key_plane = keep.tile([P, TOKENS], U8, name="key_plane", align_bytes=64)
-        val_plane = keep.tile([P, TOKENS], U8, name="val_plane", align_bytes=64)
-        nc.vector.memset(key_plane[:].bitcast(I32), 0)
-
-        def load_plane(queue, plane, scales, first_row):
-            for quad in range(4):
-                row = 32 * quad + first_row
-                queue.dma_start(plane[row:row + 4, :].bitcast(I32), scales[0, 4 * quad:4 * quad + 4, :].bitcast(I32))
-
-        def load_rows(queue, operand, name, tag):
-            raw = keep.tile([P, PACK, Q], F32, name=name, tag=tag, align_bytes=64)
-            queue.dma_start(raw[:], operand.rearrange("(p j) q -> p j q", j=PACK))
-            return raw
-
-        def load_words(words, name, tag):
-            pool_words = keep.tile([P, TOKENS], I32, name=name, tag=tag, align_bytes=64)
-            nc.sync.dma_start(pool_words[:], words[0].rearrange("p n t -> p (n t)").bitcast(I32))
-            return pool_words
-
-        age_col = keep.tile([P, HALVES, PACK], F32, name="age_col")
-        nc.sync.dma_start(age_col[:], age[0].rearrange("(h n j) -> n h j", h=HALVES, j=PACK))
-        load_plane(nc.sync, key_plane, keys_scales, 0)
-        query_raw = load_rows(nc.scalar, query, "query_raw", "gout_raw")
-        dquery_raw = load_rows(nc.scalar, dquery, "dquery_raw", "val_words")
-        rate_table = keep.tile([P, TABLE], F32, name="rate_table", tag="base_sb")
-        nc.gpsimd.dma_start(rate_table[:], ptab)
-        ones = keep.tile([P, P], F32, name="ones", tag="key_words", align_bytes=64)
-        nc.gpsimd.memset(ones[:], 1.0)
-        ident = keep.tile([P, P], F32, name="ident")
-        nc.gpsimd.affine_select(out=ident[:], in_=ones[:], compare_op=ALU.is_equal, fill=0.0, base=0,
-                                pattern=[[-1, P]], channel_multiplier=1)
-        key_words = load_words(keys_words, "key_words", "key_words")
-        nc.gpsimd.memset(val_plane[:].bitcast(I32), 0)
-        load_plane(nc.sync, val_plane, vals_scales, VAL_ROW)
-
-        def gather(window, dtype, name, first, count, tag):
-            got = keep.tile([P, count], dtype, name=name, tag=tag, align_bytes=64)
-            nc.vector.tensor_copy(got[:], window.indirect(slot_list[:, first // 16:(first + count) // 16]))
-            return got
-
-        key_scale = gather(key_plane[:], U8, "key_scale", 0, SLOTS, "key_scale")
-
-        qd_bf = keep.tile([P, 2 * Q, PACK], BF16, name="qd_bf", align_bytes=64)
-        nc.scalar.copy(qd_bf[:, 0:Q, :], query_raw[:].rearrange("p j q -> p q j"))
-        gout_raw = load_rows(nc.sync, gout, "gout_raw", "gout_raw")
-        nc.scalar.copy(qd_bf[:, Q:2 * Q, :], dquery_raw[:].rearrange("p j q -> p q j"))
-        qd_codes = keep.tile([P, 2 * Q], U32, name="qd_codes", align_bytes=64)
-        qd_scale = keep.tile([P, 2 * Q], U8, name="qd_scale", align_bytes=64)
-        nc.vector.quantize_mx(out=qd_codes[:].bitcast(FP8X4), scales=qd_scale[:],
-                              in_=qd_bf[:].rearrange("p q j -> p (q j)"))
-
-        val_words = load_words(vals_words, "val_words", "val_words")
-        log_rate = keep.tile([P, PAGES], F32, name="log_rate")
-        nc.vector.tensor_copy(log_rate[:], rate_table[:].indirect(page_list[:]))
-        rate = keep.tile([P, PAGES, PACK], F32, name="rate")
-        nc.scalar.activation(rate[:], log_rate[:].unsqueeze(2).to_broadcast([P, PAGES, PACK]), ACT.Exp)
-        base_sb = keep.tile([P, PAGES], F32, name="base_sb", tag="base_sb")
-        nc.sync.dma_start(base_sb[:], base)
-        rate_turned = psum.tile([P, HALVES, Q], F32, name="rate_turned", tag="pull0")
-        rate_quads = rate[:].rearrange("p g r -> p (g r)")
-        for h in range(HALVES):
-            nc.tensor.transpose(rate_turned[:, h, :], rate_quads[:, h * QUADS:(h + 1) * QUADS], ident[:])
-        fade = []
-        for h in range(HALVES):
-            fade_turned = keep.tile([P, PACK, Q], F32, name=f"fade_turned{h}", tag=f"fade_turned{h}", align_bytes=64)
-            fade_bank = psum.tile([P, PACK, QUADS], F32, name=f"fade_bank{h}", tag="turn", bufs=2)
-            for j in range(PACK):
-                nc.scalar.activation(fade_turned[:, j, :], rate_turned[:, h, :], ACT.Copy, scale=age_col[:, h, j:j + 1])
-                nc.tensor.transpose(fade_bank[:, j, :], fade_turned[:, j, :], ident[:])
-            fade_h = keep.tile([P, HALF], F32, name=f"fade{h}", tag=f"fade{h}", align_bytes=64)
-            nc.scalar.copy(fade_h[:].rearrange("p (n j) -> p n j", j=PACK), fade_bank[:].rearrange("p j n -> p n j"))
-            fade.append(fade_h)
-
-        age_bank = psum.tile([P, PACK, QUADS], F32, name="age_bank", tag="pull1")
-        for j in range(PACK):
-            nc.tensor.transpose(age_bank[:, j, :], age_col[:, 1, j:j + 1].to_broadcast([P, P]), ident[:])
-        age_row = keep.tile([P, HALF], F32, name="age_row")
-        nc.scalar.copy(age_row[:].rearrange("p (n j) -> p n j", j=PACK), age_bank[:].rearrange("p j n -> p n j"))
-
-        def product(name, tag, codes, scale, words, words_scale):
-            bank = psum.tile([P, HALF], F32, name=name, tag=tag)
-            nc.tensor.matmul_mx(out=bank[:], lhsT=codes.bitcast(FP8X4), lhsT_scale=scale,
-                                rhs=words[:].bitcast(FP8X4), rhs_scale=words_scale, start=True, stop=True)
-            return bank[:]
-
-        score, tangent = [], []
-        for h in range(HALVES):
-            keys_h = gather(key_words[:].bitcast(U32), U32, f"keys{h}", h * HALF, HALF, f"keys{h}")
-            cols = slice(h * HALF, (h + 1) * HALF)
-            score.append(product(f"score{h}", f"score{h}", qd_codes[:, 0:Q], qd_scale[:, 0:Q], keys_h, key_scale[:, cols]))
-            tangent.append(product(f"tangent{h}", f"tangent{h}", qd_codes[:, Q:2 * Q], qd_scale[:, Q:2 * Q], keys_h,
-                                   key_scale[:, cols]))
-
-        def slots_tile(name):
+        def half_tile(name):
             return keep.tile([P, HALF], F32, name=name)
 
         def column(name):
             return keep.tile([P, 1], F32, name=name)
 
-        logit = [slots_tile(f"logit{h}") for h in range(HALVES)]
-        weight = [slots_tile(f"weight{h}") for h in range(HALVES)]
-        cool_sum = [column(f"cool_sum{h}") for h in range(HALVES)]
+        def load_rows(queue, operand, name):
+            raw = shared([P, PACK, Q], F32, name, name)
+            queue.dma_start(raw[:], operand.rearrange("(p t) q -> p t q", t=PACK))
+            return raw
+
+        def load_words(words, name):
+            stored = shared([P, TOKENS], I32, name, name)
+            nc.sync.dma_start(stored[:], words[0].rearrange("p c t -> p (c t)").bitcast(I32))
+            return stored
+
+        def gather(window, dtype, name, first, count, tag):
+            picked = shared([P, count], dtype, name, tag)
+            entries = slot_list[:, first // LIST_COLUMN:(first + count) // LIST_COLUMN]
+            nc.vector.tensor_copy(picked[:], window.indirect(entries))
+            return picked
+
+        def product(name, codes, scale, words, words_scale):
+            bank = psum.tile([P, HALF], F32, name=name, tag=name)
+            nc.tensor.matmul_mx(out=bank[:], lhsT=codes.bitcast(FP8X4), lhsT_scale=scale,
+                                rhs=words[:].bitcast(FP8X4), rhs_scale=words_scale, start=True, stop=True)
+            return bank[:]
+
+        def aged_quad_sums(values, h, sums, name):
+            turned = psum.tile([P, QUAD, Q], F32, name=name + "_turned", tag="turn", bufs=2)
+            for j in range(QUAD):
+                nc.tensor.transpose(turned[:, j, :], values[:].rearrange("p (n j) -> p j n", j=QUAD)[:, j, :], ident[:])
+            aged = keep.tile([P, QUAD, Q], F32, name=name + "_aged")
+            for j in range(QUAD):
+                nc.scalar.activation(aged[:, j, :], turned[:, j, :], ACT.Copy, scale=age_col[:, h, j:j + 1])
+            for j in range(QUAD):
+                nc.tensor.matmul(sums, lhsT=aged[:, j, :], rhs=ident[:], is_transpose=True,
+                                 start=(j == 0), stop=(j == QUAD - 1))
+
+        slot_list = keep.tile([P, SLOTS // LIST_COLUMN], U16, name="slot_list")
+        page_list = keep.tile([P, PAGES // LIST_COLUMN], U16, name="page_list")
+        nc.sync.dma_start(slot_list[:], offs)
+        nc.sync.dma_start(page_list[:], offs2)
+
+        key_plane = keep.tile([P, TOKENS], U8, name="key_plane", align_bytes=MX_ALIGN)
+        val_rows = keep.tile([P, TOKENS], U8, name="val_rows", align_bytes=MX_ALIGN)
+        nc.vector.memset(key_plane[:].bitcast(I32), 0)
+        nc.gpsimd.memset(val_rows[:].bitcast(I32), 0)
+
+        age_col = keep.tile([P, HALVES, QUAD], F32, name="age_col")
+        nc.sync.dma_start(age_col[:], age[0].rearrange("(h n j) -> n h j", h=HALVES, j=QUAD))
+        for r in range(QUADRANT_ROWS):
+            nc.sync.dma_start(key_plane[r:P:QUADRANT, :].bitcast(I32),
+                              keys_scales[0, r:SCALE_ROWS:QUADRANT_ROWS, :].bitcast(I32))
+        nc.sync.dma_start(val_rows[0:P:SPREAD, :].bitcast(I32), vals_scales[0].bitcast(I32))
+        query_raw = load_rows(nc.scalar, query, "query_raw")
+        dquery_raw = load_rows(nc.scalar, dquery, "dquery_raw")
+        rate_table = keep.tile([P, TABLE], F32, name="rate_table")
+        nc.scalar.dma_start(rate_table[:], ptab)
+
+        ones = shared([P, P], F32, "ones", "key_words")
+        nc.gpsimd.memset(ones[:], 1.0)
+        ident = keep.tile([P, P], F32, name="ident")
+        nc.gpsimd.affine_select(out=ident[:], in_=ones[:], compare_op=ALU.is_equal, fill=0.0, base=0,
+                                pattern=[[-1, P]], channel_multiplier=1)
+        key_words = load_words(keys_words, "key_words")
+
+        key_scale = gather(key_plane[:], U8, "key_scale", 0, SLOTS, "key_scale")
+        val_picked = gather(val_rows[:], U8, "val_picked", 0, SLOTS, "val_picked")
+
+        pair_bf = keep.tile([P, 2 * Q, PACK], BF16, name="pair_bf", align_bytes=MX_ALIGN)
+        nc.scalar.copy(pair_bf[:, 0:Q, :], query_raw[:].rearrange("p t q -> p q t"))
+        nc.scalar.copy(pair_bf[:, Q:2 * Q, :], dquery_raw[:].rearrange("p t q -> p q t"))
+        pair_codes = keep.tile([P, 2 * Q], U32, name="pair_codes", align_bytes=MX_ALIGN)
+        pair_scale = keep.tile([P, 2 * Q], U8, name="pair_scale", align_bytes=MX_ALIGN)
+        nc.vector.quantize_mx(out=pair_codes[:].bitcast(FP8X4), scales=pair_scale[:],
+                              in_=pair_bf[:].rearrange("p q t -> p (q t)"))
+
+        log_rate = keep.tile([P, PAGES], F32, name="log_rate")
+        nc.vector.tensor_copy(log_rate[:], rate_table[:].indirect(page_list[:]))
+        rate = shared([P, PAGES, PAGE_QUADS], F32, "rate", "gout_raw")
+        nc.scalar.activation(rate[:], log_rate[:].unsqueeze(2).to_broadcast([P, PAGES, PAGE_QUADS]), ACT.Exp)
+        rate_turned = psum.tile([P, HALVES, Q], F32, name="rate_turned", tag="pull0")
+        rate_quads = rate[:].rearrange("p g r -> p (g r)")
+        for h in range(HALVES):
+            nc.tensor.transpose(rate_turned[:, h, :], rate_quads[:, h * QUADS:(h + 1) * QUADS], ident[:])
+        gout_raw = load_rows(nc.sync, gout, "gout_raw")
+        fade = []
+        for h, next_tenant in enumerate(("val_words", "gout_bf")):
+            fade_turned = shared([P, QUAD, Q], F32, f"fade_turned{h}", next_tenant)
+            fade_bank = psum.tile([P, QUAD, QUADS], F32, name=f"fade_bank{h}", tag="turn", bufs=2)
+            for j in range(QUAD):
+                nc.scalar.activation(fade_turned[:, j, :], rate_turned[:, h, :], ACT.Copy, scale=age_col[:, h, j:j + 1])
+                nc.tensor.transpose(fade_bank[:, j, :], fade_turned[:, j, :], ident[:])
+            fade_h = shared([P, HALF], F32, f"fade{h}", f"fade{h}")
+            nc.scalar.copy(fade_h[:].rearrange("p (n j) -> p n j", j=QUAD), fade_bank[:].rearrange("p j n -> p n j"))
+            fade.append(fade_h)
+
+        val_words = load_words(vals_words, "val_words")
+        gout_bf = shared([P, Q, PACK], BF16, "gout_bf", "gout_bf")
+        nc.scalar.copy(gout_bf[:], gout_raw[:].rearrange("p t q -> p q t"))
+        val_scale = shared([P, SLOTS], U8, "val_scale", "gout_raw")
+        nc.gpsimd.memset(val_scale[:].bitcast(I32), 0)
+        for r in range(QUADRANT_ROWS):
+            nc.sync.dma_start(val_scale[r:P:QUADRANT, :].bitcast(I32), val_picked[SPREAD * r:P:QUADRANT, :].bitcast(I32))
+
+        last = HALVES - 1
+        age_bank = psum.tile([P, QUAD, QUADS], F32, name="age_bank", tag="pull1")
+        for j in range(QUAD):
+            nc.tensor.transpose(age_bank[:, j, :], age_col[:, last, j:j + 1].to_broadcast([P, P]), ident[:])
+        age_row = half_tile("age_row")
+        nc.scalar.copy(age_row[:].rearrange("p (n j) -> p n j", j=QUAD), age_bank[:].rearrange("p j n -> p n j"))
+
+        keys = [gather(key_words[:].bitcast(U32), U32, f"keys{h}", h * HALF, HALF, f"keys{h}") for h in range(HALVES)]
+        score = [product(f"score{h}", pair_codes[:, 0:Q], pair_scale[:, 0:Q], keys[h],
+                         key_scale[:, h * HALF:(h + 1) * HALF]) for h in range(HALVES)]
+        tangent = [product(f"tangent{h}", pair_codes[:, Q:2 * Q], pair_scale[:, Q:2 * Q], keys[h],
+                           key_scale[:, h * HALF:(h + 1) * HALF]) for h in range(HALVES)]
+
+        logit = [half_tile(f"logit{h}") for h in range(HALVES)]
+        weight = [half_tile(f"weight{h}") for h in range(HALVES)]
+        cool_part = [column(f"cool_part{h}") for h in range(HALVES)]
         for h in range(HALVES):
             nc.vector.tensor_tensor(logit[h][:], score[h], fade[h][:], ALU.subtract)
-            nc.scalar.activation(weight[h][:], logit[h][:], ACT.Exp, scale=1.0 / COOL, accum_out=cool_sum[h][:])
+            nc.scalar.activation(weight[h][:], logit[h][:], ACT.Exp, scale=1.0 / COOL, accum_out=cool_part[h][:])
 
-        gout_bf = keep.tile([P, Q, PACK], BF16, name="gout_bf", tag="fade_turned1", align_bytes=64)
-        nc.scalar.copy(gout_bf[:], gout_raw[:].rearrange("p j q -> p q j"))
-        gout_codes = keep.tile([P, Q], U32, name="gout_codes", tag="keys0", align_bytes=64)
-        gout_scale = keep.tile([P, Q], U8, name="gout_scale", align_bytes=64)
+        gout_codes = shared([P, Q], U32, "gout_codes", "keys0")
+        gout_scale = keep.tile([P, Q], U8, name="gout_scale", align_bytes=MX_ALIGN)
         nc.vector.quantize_mx(out=gout_codes[:].bitcast(FP8X4), scales=gout_scale[:],
-                              in_=gout_bf[:].rearrange("p q j -> p (q j)"))
+                              in_=gout_bf[:].rearrange("p q t -> p (q t)"))
 
-        val_scale = gather(val_plane[:], U8, "val_scale", 0, SLOTS, "fade1")
+        base_sb = shared([P, PAGES], F32, "base_sb", "fade0")
+        nc.sync.dma_start(base_sb[:], base)
 
-        cool_total = keep.tile([P, 1], F32, name="cool_total", tag="vals0", align_bytes=64)
-        nc.scalar.activation(cool_total[:], cool_sum[0][:], ACT.Identity, bias=cool_sum[1][:])
-        shift = keep.tile([P, 1], F32, name="shift", tag="vals1", align_bytes=64)
-        nc.scalar.activation(shift[:], cool_total[:].bitcast(U32), ACT.Copy,
+        cool_sum = shared([P, 1], F32, "cool_sum", "vals1")
+        nc.scalar.activation(cool_sum[:], cool_part[0][:], ACT.Identity, bias=cool_part[1][:])
+        shift = column("shift")
+        nc.scalar.activation(shift[:], cool_sum[:].bitcast(U32), ACT.Copy,
                              scale=-COOL * math.log(2.0) / 2.0 ** 23,
                              bias=COOL * (127.0 * math.log(2.0) + 0.5 * math.log(SLOTS)))
         norm_part = [column(f"norm_part{h}") for h in range(HALVES)]
@@ -171,31 +197,19 @@ def tile_attend_hvpagerate_kernel(tc, query, keys_words, keys_scales, ptab, age,
         norm = column("norm")
         nc.scalar.activation(norm[:], norm_part[0][:], ACT.Identity, bias=norm_part[1][:])
 
-        def aged_quad_sums(values, h, sums, name):
-            turned = psum.tile([P, PACK, Q], F32, name=name + "_turned", tag="turn", bufs=2)
-            for j in range(PACK):
-                nc.tensor.transpose(turned[:, j, :], values[:].rearrange("p (n j) -> p j n", j=PACK)[:, j, :], ident[:])
-            aged = keep.tile([P, PACK, Q], F32, name=name + "_aged")
-            for j in range(PACK):
-                nc.scalar.activation(aged[:, j, :], turned[:, j, :], ACT.Copy, scale=age_col[:, h, j:j + 1])
-            for j in range(PACK):
-                nc.tensor.matmul(sums, lhsT=aged[:, j, :], rhs=ident[:], is_transpose=True,
-                                 start=(j == 0), stop=(j == PACK - 1))
-
         pull = []
-        for h in range(HALVES):
-            vals_h = gather(val_words[:].bitcast(U32), U32, f"vals{h}", h * HALF, HALF, f"vals{h}")
-            pull.append(product(f"pull{h}", f"pull{h}", gout_codes[:], gout_scale[:], vals_h,
-                                val_scale[VAL_ROW:P, h * HALF:(h + 1) * HALF]))
+        for h, earlier_tenant in enumerate(("fade1", "vals1")):
+            vals_h = gather(val_words[:].bitcast(U32), U32, f"vals{h}", h * HALF, HALF, earlier_tenant)
+            pull.append(product(f"pull{h}", gout_codes[:], gout_scale[:], vals_h, val_scale[:, h * HALF:(h + 1) * HALF]))
 
-        early_sums = psum.tile([P, HALVES, QUADS], F32, name="early_sums", tag="score0")
+        weight_quads = psum.tile([P, HALVES, QUADS], F32, name="weight_quads", tag="score0")
         for h in range(HALVES):
-            aged_quad_sums(weight[h], h, early_sums[:, h, :], f"weight{h}")
+            aged_quad_sums(weight[h], h, weight_quads[:, h, :], f"weight{h}")
 
-        cross = [slots_tile(f"cross{h}") for h in range(HALVES)]
+        cross = [half_tile(f"cross{h}") for h in range(HALVES)]
         tangent_part = [column(f"tangent_part{h}") for h in range(HALVES)]
         pull_part = [column(f"pull_part{h}") for h in range(HALVES)]
-        cov_part = [column(f"cov_part{h}") for h in range(HALVES)]
+        cross_part = [column(f"cross_part{h}") for h in range(HALVES)]
         for h in range(HALVES):
             nc.vector.scalar_tensor_tensor(logit[h][:], weight[h][:], 1.0, tangent[h], ALU.mult, ALU.mult,
                                            accum_out=tangent_part[h][:])
@@ -210,30 +224,33 @@ def tile_attend_hvpagerate_kernel(tc, query, keys_words, keys_scales, ptab, age,
         nc.vector.tensor_scalar(pull_mean[:], pull_part[0][:], pull_part[1][:], inv_norm[:], ALU.add, ALU.mult)
         out_factor = column("out_factor")
         nc.scalar.activation(out_factor[:], inv_norm[:], ACT.Copy, scale=-OUT_SCALE)
+        cov_scale = column("cov_scale")
+        nc.scalar.activation(cov_scale[:], inv_norm[:], ACT.Copy, scale=out_factor[:])
 
-        late_sums = psum.tile([P, QUADS], F32, name="late_sums", tag="score1")
-        late_pages = keep.tile([P, PAGES], F32, name="late_pages")
+        cross_quads = psum.tile([P, QUADS], F32, name="cross_quads", tag="score1")
+        cross_pages = keep.tile([P, PAGES], F32, name="cross_pages")
         for h in range(HALVES):
             centred = keep.tile([P, HALF], F32, name=f"centred{h}", tag="centred")
             nc.vector.scalar_tensor_tensor(centred[:], tangent[h], tangent_mean[:], weight[h][:],
                                            ALU.subtract, ALU.mult)
             nc.vector.scalar_tensor_tensor(cross[h][:], pull[h], pull_mean[:], centred[:], ALU.subtract, ALU.mult,
-                                           accum_out=cov_part[h][:])
-        aged_quad_sums(cross[0], 0, late_sums[:], "cross0")
-        nc.vector.tensor_tensor(logit[1][:], cross[1][:], age_row[:], ALU.mult)
-        nc.vector.tensor_reduce(late_pages[:, HALF_PAGES:PAGES], logit[1][:].rearrange("p (g s) -> p g s", s=16),
+                                           accum_out=cross_part[h][:])
+        aged_quad_sums(cross[0], 0, cross_quads[:], "cross0")
+        aged_cross = logit[last]
+        nc.vector.tensor_tensor(aged_cross[:], cross[last][:], age_row[:], ALU.mult)
+        nc.vector.tensor_reduce(cross_pages[:, HALF_PAGES:PAGES], aged_cross[:].rearrange("p (g s) -> p g s", s=PAGE),
                                 AXIS.X, ALU.add)
 
-        early_pages = keep.tile([P, PAGES], F32, name="early_pages")
-        nc.vector.tensor_reduce(early_pages[:], early_sums[:].rearrange("p h (g r) -> p (h g) r", r=PACK), AXIS.X, ALU.add)
-        covariance = column("covariance")
-        nc.vector.tensor_scalar(covariance[:], cov_part[0][:], cov_part[1][:], inv_norm[:], ALU.add, ALU.mult)
-        spread = keep.tile([P, PAGES], F32, name="spread")
-        nc.vector.tensor_scalar(spread[:], early_pages[:], covariance[:], out_factor[:], ALU.mult, ALU.mult)
-        rest = keep.tile([P, PAGES], F32, name="rest")
-        nc.vector.tensor_tensor(rest[:], base_sb[:], spread[:], ALU.subtract)
+        weight_pages = keep.tile([P, PAGES], F32, name="weight_pages")
+        nc.vector.tensor_reduce(weight_pages[:], weight_quads[:].rearrange("p h (g r) -> p (h g) r", r=PAGE_QUADS),
+                                AXIS.X, ALU.add)
+        cov_factor = column("cov_factor")
+        nc.vector.tensor_scalar(cov_factor[:], cross_part[0][:], cross_part[1][:], cov_scale[:], ALU.add, ALU.mult)
+        minus_rest = keep.tile([P, PAGES], F32, name="minus_rest")
+        nc.vector.scalar_tensor_tensor(minus_rest[:], weight_pages[:], cov_factor[:], base_sb[:], ALU.mult, ALU.subtract)
 
-        nc.vector.tensor_reduce(late_pages[:, 0:HALF_PAGES], late_sums[:].rearrange("p (g r) -> p g r", r=PACK), AXIS.X, ALU.add)
+        nc.vector.tensor_reduce(cross_pages[:, 0:HALF_PAGES], cross_quads[:].rearrange("p (g r) -> p g r", r=PAGE_QUADS),
+                                AXIS.X, ALU.add)
         result = keep.tile([P, PAGES], F32, name="result")
-        nc.vector.scalar_tensor_tensor(result[:], late_pages[:], out_factor[:], rest[:], ALU.mult, ALU.add)
+        nc.vector.scalar_tensor_tensor(result[:], cross_pages[:], out_factor[:], minus_rest[:], ALU.mult, ALU.subtract)
         nc.sync.dma_start(out, result[:])

@@ -52,7 +52,7 @@ def tile_attend_hvpagerate_kernel(tc, query, keys_words, keys_scales, ptab, age,
             return keep.tile(shape, dtype, name=name, tag=tag, align_bytes=MX_ALIGN)
 
         def half_tile(name):
-            return keep.tile([P, HALF], F32, name=name)
+            return keep.tile([P, QUAD, QUADS], F32, name=name)
 
         def column(name):
             return keep.tile([P, 1], F32, name=name)
@@ -77,12 +77,12 @@ def tile_attend_hvpagerate_kernel(tc, query, keys_words, keys_scales, ptab, age,
             bank = psum.tile([P, HALF], F32, name=name, tag=name)
             nc.tensor.matmul_mx(out=bank[:], lhsT=codes.bitcast(FP8X4), lhsT_scale=scale,
                                 rhs=words[:].bitcast(FP8X4), rhs_scale=words_scale, start=True, stop=True)
-            return bank[:]
+            return bank[:].rearrange("p (n j) -> p j n", j=QUAD)
 
         def aged_quad_sums(values, h, sums, name):
             turned = psum.tile([P, QUAD, Q], F32, name=name + "_turned", tag="turn", bufs=2)
             for j in range(QUAD):
-                nc.tensor.transpose(turned[:, j, :], values[:].rearrange("p (n j) -> p j n", j=QUAD)[:, j, :], ident[:])
+                nc.tensor.transpose(turned[:, j, :], values[:, j, :], ident[:])
             aged = keep.tile([P, QUAD, Q], F32, name=name + "_aged")
             for j in range(QUAD):
                 nc.scalar.activation(aged[:, j, :], turned[:, j, :], ACT.Copy, scale=age_col[:, h, j:j + 1])
@@ -145,8 +145,8 @@ def tile_attend_hvpagerate_kernel(tc, query, keys_words, keys_scales, ptab, age,
             for j in range(QUAD):
                 nc.scalar.activation(fade_turned[:, j, :], rate_turned[:, h, :], ACT.Copy, scale=age_col[:, h, j:j + 1])
                 nc.tensor.transpose(fade_bank[:, j, :], fade_turned[:, j, :], ident[:])
-            fade_h = shared([P, HALF], F32, f"fade{h}", f"fade{h}")
-            nc.scalar.copy(fade_h[:].rearrange("p (n j) -> p n j", j=QUAD), fade_bank[:].rearrange("p j n -> p n j"))
+            fade_h = shared([P, QUAD, QUADS], F32, f"fade{h}", f"fade{h}")
+            nc.scalar.copy(fade_h[:], fade_bank[:])
             fade.append(fade_h)
 
         val_words = load_words(vals_words, "val_words")
@@ -162,7 +162,7 @@ def tile_attend_hvpagerate_kernel(tc, query, keys_words, keys_scales, ptab, age,
         for j in range(QUAD):
             nc.tensor.transpose(age_bank[:, j, :], age_col[:, last, j:j + 1].to_broadcast([P, P]), ident[:])
         age_row = half_tile("age_row")
-        nc.scalar.copy(age_row[:].rearrange("p (n j) -> p n j", j=QUAD), age_bank[:].rearrange("p j n -> p n j"))
+        nc.scalar.copy(age_row[:], age_bank[:])
 
         keys = [gather(key_words[:].bitcast(U32), U32, f"keys{h}", h * HALF, HALF, f"keys{h}") for h in range(HALVES)]
         score = [product(f"score{h}", pair_codes[:, 0:Q], pair_scale[:, 0:Q], keys[h],
@@ -206,48 +206,58 @@ def tile_attend_hvpagerate_kernel(tc, query, keys_words, keys_scales, ptab, age,
         for h in range(HALVES):
             aged_quad_sums(weight[h], h, weight_quads[:, h, :], f"weight{h}")
 
-        cross = [half_tile(f"cross{h}") for h in range(HALVES)]
-        tangent_part = [column(f"tangent_part{h}") for h in range(HALVES)]
-        pull_part = [column(f"pull_part{h}") for h in range(HALVES)]
-        cross_part = [column(f"cross_part{h}") for h in range(HALVES)]
+        moved = [half_tile(f"moved{h}") for h in range(HALVES)]
+        pulled = [half_tile(f"pulled{h}") for h in range(HALVES)]
+        moved_part = [column(f"moved_part{h}") for h in range(HALVES)]
+        pulled_part = [column(f"pulled_part{h}") for h in range(HALVES)]
         for h in range(HALVES):
-            nc.vector.scalar_tensor_tensor(logit[h][:], weight[h][:], 1.0, tangent[h], ALU.mult, ALU.mult,
-                                           accum_out=tangent_part[h][:])
+            nc.vector.scalar_tensor_tensor(moved[h][:], weight[h][:], 1.0, tangent[h], ALU.mult, ALU.mult,
+                                           accum_out=moved_part[h][:])
         inv_norm = column("inv_norm")
         nc.vector.reciprocal(inv_norm[:], norm[:])
+        pulled_quads = psum.tile([P, HALVES, QUADS], F32, name="pulled_quads", tag="score1")
         for h in range(HALVES):
-            nc.vector.scalar_tensor_tensor(cross[h][:], weight[h][:], 1.0, pull[h], ALU.mult, ALU.mult,
-                                           accum_out=pull_part[h][:])
-        tangent_mean = column("tangent_mean")
-        nc.vector.tensor_scalar(tangent_mean[:], tangent_part[0][:], tangent_part[1][:], inv_norm[:], ALU.add, ALU.mult)
+            nc.vector.scalar_tensor_tensor(pulled[h][:], weight[h][:], 1.0, pull[h], ALU.mult, ALU.mult,
+                                           accum_out=pulled_part[h][:])
+            aged_quad_sums(pulled[h], h, pulled_quads[:, h, :], f"pulled{h}")
         pull_mean = column("pull_mean")
-        nc.vector.tensor_scalar(pull_mean[:], pull_part[0][:], pull_part[1][:], inv_norm[:], ALU.add, ALU.mult)
+        nc.vector.tensor_scalar(pull_mean[:], pulled_part[0][:], pulled_part[1][:], inv_norm[:], ALU.add, ALU.mult)
         out_factor = column("out_factor")
-        nc.scalar.activation(out_factor[:], inv_norm[:], ACT.Copy, scale=-OUT_SCALE)
+        nc.vector.tensor_scalar(out_factor[:], inv_norm[:], -OUT_SCALE, None, ALU.mult)
         cov_scale = column("cov_scale")
-        nc.scalar.activation(cov_scale[:], inv_norm[:], ACT.Copy, scale=out_factor[:])
+        nc.vector.tensor_scalar(cov_scale[:], inv_norm[:], -OUT_SCALE, inv_norm[:], ALU.mult, ALU.mult)
+        pulled_factor = column("pulled_factor")
+        nc.vector.tensor_scalar(pulled_factor[:], moved_part[0][:], moved_part[1][:], cov_scale[:], ALU.add, ALU.mult)
 
-        cross_quads = psum.tile([P, QUADS], F32, name="cross_quads", tag="score1")
+        cross = [half_tile(f"cross{h}") for h in range(HALVES)]
+        cross_part = [column(f"cross_part{h}") for h in range(HALVES)]
+        cross_quads = psum.tile([P, QUADS], F32, name="cross_quads", tag="tangent0")
         cross_pages = keep.tile([P, PAGES], F32, name="cross_pages")
         for h in range(HALVES):
-            centred = keep.tile([P, HALF], F32, name=f"centred{h}", tag="centred")
-            nc.vector.scalar_tensor_tensor(centred[:], tangent[h], tangent_mean[:], weight[h][:],
-                                           ALU.subtract, ALU.mult)
-            nc.vector.scalar_tensor_tensor(cross[h][:], pull[h], pull_mean[:], centred[:], ALU.subtract, ALU.mult,
+            nc.vector.scalar_tensor_tensor(cross[h][:], pull[h], pull_mean[:], moved[h][:], ALU.subtract, ALU.mult,
                                            accum_out=cross_part[h][:])
         aged_quad_sums(cross[0], 0, cross_quads[:], "cross0")
-        aged_cross = logit[last]
+        aged_cross = half_tile("aged_cross")
         nc.vector.tensor_tensor(aged_cross[:], cross[last][:], age_row[:], ALU.mult)
-        nc.vector.tensor_reduce(cross_pages[:, HALF_PAGES:PAGES], aged_cross[:].rearrange("p (g s) -> p g s", s=PAGE),
-                                AXIS.X, ALU.add)
+        nc.vector.tensor_reduce(cross_pages[:, HALF_PAGES:PAGES],
+                                aged_cross[:].rearrange("p j (g r) -> p g j r", r=PAGE_QUADS), AXIS.XY, ALU.add)
 
-        weight_pages = keep.tile([P, PAGES], F32, name="weight_pages")
-        nc.vector.tensor_reduce(weight_pages[:], weight_quads[:].rearrange("p h (g r) -> p (h g) r", r=PAGE_QUADS),
-                                AXIS.X, ALU.add)
+        def page_sums(quads, name):
+            pages = keep.tile([P, PAGES], F32, name=name)
+            nc.vector.tensor_reduce(pages[:], quads[:].rearrange("p h (g r) -> p (h g) r", r=PAGE_QUADS), AXIS.X, ALU.add)
+            return pages
+
+        weight_pages = page_sums(weight_quads, "weight_pages")
         cov_factor = column("cov_factor")
         nc.vector.tensor_scalar(cov_factor[:], cross_part[0][:], cross_part[1][:], cov_scale[:], ALU.add, ALU.mult)
+        weight_factor = column("weight_factor")
+        nc.vector.tensor_scalar(weight_factor[:], pulled_factor[:], pull_mean[:], cov_factor[:], ALU.mult, ALU.subtract)
+        with_weight = keep.tile([P, PAGES], F32, name="with_weight")
+        nc.vector.scalar_tensor_tensor(with_weight[:], weight_pages[:], weight_factor[:], base_sb[:], ALU.mult, ALU.add)
+        pulled_pages = page_sums(pulled_quads, "pulled_pages")
         minus_rest = keep.tile([P, PAGES], F32, name="minus_rest")
-        nc.vector.scalar_tensor_tensor(minus_rest[:], weight_pages[:], cov_factor[:], base_sb[:], ALU.mult, ALU.subtract)
+        nc.vector.scalar_tensor_tensor(minus_rest[:], pulled_pages[:], pulled_factor[:], with_weight[:],
+                                       ALU.mult, ALU.subtract)
 
         nc.vector.tensor_reduce(cross_pages[:, 0:HALF_PAGES], cross_quads[:].rearrange("p (g r) -> p g r", r=PAGE_QUADS),
                                 AXIS.X, ALU.add)

import math
from contextlib import ExitStack

import concourse.mybir as mybir

F32 = mybir.dt.float32
BF16 = mybir.dt.bfloat16
I32 = mybir.dt.int32
U32 = mybir.dt.uint32
U16 = mybir.dt.uint16
U8 = mybir.dt.uint8
FP8X4 = mybir.dt.float8_e4m3fn_x4
ALU = mybir.AluOpType
ACT = mybir.ActivationFunctionType
AXIS = mybir.AxisListType

P = 128
Q = 128
FEATURES = 512
PACK = 4
TOKENS = 4096
TABLE = 512
SLOTS = 1024
PAGES = 64
PAGE = SLOTS // PAGES
LIST_COLUMN = 16
HALVES = 2
HALF = SLOTS // HALVES
HALF_PAGES = PAGES // HALVES
QUAD = 4
QUADS = HALF // QUAD
PAGE_QUADS = PAGE // QUAD
SCALE_ROWS = 16
QUADRANT = 32
QUADRANT_ROWS = 4
SPREAD = P // SCALE_ROWS
MX_ALIGN = 64
COOL = 8.0
OUT_SCALE = 64.0

FLOPS = 3 * 2 * FEATURES * Q * SLOTS


def tile_attend_hvpagerate_kernel(tc, query, keys_words, keys_scales, ptab, age, gout, vals_words, vals_scales,
                                   dquery, base, offs, offs2, out):
    nc = tc.nc
    with ExitStack() as ctx:
        keep = ctx.enter_context(tc.tile_pool(name="keep", bufs=1))
        psum = ctx.enter_context(tc.psum_pool(name="psum", bufs=1))

        def shared(shape, dtype, name, tag):
            return keep.tile(shape, dtype, name=name, tag=tag, align_bytes=MX_ALIGN)

        def half_tile(name):
            return keep.tile([P, QUAD, QUADS], F32, name=name)

        def column(name):
            return keep.tile([P, 1], F32, name=name)

        def load_rows(queue, operand, name):
            raw = shared([P, PACK, Q], F32, name, name)
            queue.dma_start(raw[:], operand.rearrange("(p t) q -> p t q", t=PACK))
            return raw

        def load_words(words, name):
            stored = shared([P, TOKENS], I32, name, name)
            nc.sync.dma_start(stored[:], words[0].rearrange("p c t -> p (c t)").bitcast(I32))
            return stored

        def gather(window, dtype, name, first, count, tag):
            picked = shared([P, count], dtype, name, tag)
            entries = slot_list[:, first // LIST_COLUMN:(first + count) // LIST_COLUMN]
            nc.vector.tensor_copy(picked[:], window.indirect(entries))
            return picked

        def product(name, codes, scale, words, words_scale):
            bank = psum.tile([P, HALF], F32, name=name, tag=name)
            nc.tensor.matmul_mx(out=bank[:], lhsT=codes.bitcast(FP8X4), lhsT_scale=scale,
                                rhs=words[:].bitcast(FP8X4), rhs_scale=words_scale, start=True, stop=True)
            return bank[:].rearrange("p (n j) -> p j n", j=QUAD)

        def aged_quad_sums(values, h, sums, name):
            turned = psum.tile([P, QUAD, Q], F32, name=name + "_turned", tag="turn", bufs=2)
            for j in range(QUAD):
                nc.tensor.transpose(turned[:, j, :], values[:, j, :], ident[:])
            aged = keep.tile([P, QUAD, Q], F32, name=name + "_aged")
            for j in range(QUAD):
                nc.scalar.activation(aged[:, j, :], turned[:, j, :], ACT.Copy, scale=age_col[:, h, j:j + 1])
            for j in range(QUAD):
                nc.tensor.matmul(sums, lhsT=aged[:, j, :], rhs=ident[:], is_transpose=True,
                                 start=(j == 0), stop=(j == QUAD - 1))

        slot_list = keep.tile([P, SLOTS // LIST_COLUMN], U16, name="slot_list")
        page_list = keep.tile([P, PAGES // LIST_COLUMN], U16, name="page_list")
        nc.sync.dma_start(slot_list[:], offs)
        nc.sync.dma_start(page_list[:], offs2)

        key_plane = keep.tile([P, TOKENS], U8, name="key_plane", align_bytes=MX_ALIGN)
        val_rows = keep.tile([P, TOKENS], U8, name="val_rows", align_bytes=MX_ALIGN)
        nc.vector.memset(key_plane[:].bitcast(I32), 0)
        nc.gpsimd.memset(val_rows[:].bitcast(I32), 0)

        age_col = keep.tile([P, HALVES, QUAD], F32, name="age_col")
        nc.sync.dma_start(age_col[:], age[0].rearrange("(h n j) -> n h j", h=HALVES, j=QUAD))
        for r in range(QUADRANT_ROWS):
            nc.sync.dma_start(key_plane[r:P:QUADRANT, :].bitcast(I32),
                              keys_scales[0, r:SCALE_ROWS:QUADRANT_ROWS, :].bitcast(I32))
        nc.sync.dma_start(val_rows[0:P:SPREAD, :].bitcast(I32), vals_scales[0].bitcast(I32))
        query_raw = load_rows(nc.scalar, query, "query_raw")
        dquery_raw = load_rows(nc.scalar, dquery, "dquery_raw")
        rate_table = keep.tile([P, TABLE], F32, name="rate_table")
        nc.scalar.dma_start(rate_table[:], ptab)

        ones = shared([P, P], F32, "ones", "key_words")
        nc.gpsimd.memset(ones[:], 1.0)
        ident = keep.tile([P, P], F32, name="ident")
        nc.gpsimd.affine_select(out=ident[:], in_=ones[:], compare_op=ALU.is_equal, fill=0.0, base=0,
                                pattern=[[-1, P]], channel_multiplier=1)
        key_words = load_words(keys_words, "key_words")

        key_scale = gather(key_plane[:], U8, "key_scale", 0, SLOTS, "key_scale")
        val_picked = gather(val_rows[:], U8, "val_picked", 0, SLOTS, "val_picked")

        pair_bf = keep.tile([P, 2 * Q, PACK], BF16, name="pair_bf", align_bytes=MX_ALIGN)
        nc.scalar.copy(pair_bf[:, 0:Q, :], query_raw[:].rearrange("p t q -> p q t"))
        nc.scalar.copy(pair_bf[:, Q:2 * Q, :], dquery_raw[:].rearrange("p t q -> p q t"))
        pair_codes = keep.tile([P, 2 * Q], U32, name="pair_codes", align_bytes=MX_ALIGN)
        pair_scale = keep.tile([P, 2 * Q], U8, name="pair_scale", align_bytes=MX_ALIGN)
        nc.vector.quantize_mx(out=pair_codes[:].bitcast(FP8X4), scales=pair_scale[:],
                              in_=pair_bf[:].rearrange("p q t -> p (q t)"))

        log_rate = keep.tile([P, PAGES], F32, name="log_rate")
        nc.vector.tensor_copy(log_rate[:], rate_table[:].indirect(page_list[:]))
        rate = shared([P, PAGES, PAGE_QUADS], F32, "rate", "gout_raw")
        nc.scalar.activation(rate[:], log_rate[:].unsqueeze(2).to_broadcast([P, PAGES, PAGE_QUADS]), ACT.Exp)
        rate_turned = psum.tile([P, HALVES, Q], F32, name="rate_turned", tag="pull0")
        rate_quads = rate[:].rearrange("p g r -> p (g r)")
        for h in range(HALVES):
            nc.tensor.transpose(rate_turned[:, h, :], rate_quads[:, h * QUADS:(h + 1) * QUADS], ident[:])
        gout_raw = load_rows(nc.sync, gout, "gout_raw")
        fade = []
        for h, next_tenant in enumerate(("val_words", "gout_bf")):
            fade_turned = shared([P, QUAD, Q], F32, f"fade_turned{h}", next_tenant)
            fade_bank = psum.tile([P, QUAD, QUADS], F32, name=f"fade_bank{h}", tag="turn", bufs=2)
            for j in range(QUAD):
                nc.scalar.activation(fade_turned[:, j, :], rate_turned[:, h, :], ACT.Copy, scale=age_col[:, h, j:j + 1])
                nc.tensor.transpose(fade_bank[:, j, :], fade_turned[:, j, :], ident[:])
            fade_h = shared([P, QUAD, QUADS], F32, f"fade{h}", f"fade{h}")
            nc.scalar.copy(fade_h[:], fade_bank[:])
            fade.append(fade_h)

        val_words = load_words(vals_words, "val_words")
        gout_bf = shared([P, Q, PACK], BF16, "gout_bf", "gout_bf")
        nc.scalar.copy(gout_bf[:], gout_raw[:].rearrange("p t q -> p q t"))
        val_scale = shared([P, SLOTS], U8, "val_scale", "gout_raw")
        nc.gpsimd.memset(val_scale[:].bitcast(I32), 0)
        for r in range(QUADRANT_ROWS):
            nc.sync.dma_start(val_scale[r:P:QUADRANT, :].bitcast(I32), val_picked[SPREAD * r:P:QUADRANT, :].bitcast(I32))

        last = HALVES - 1
        age_bank = psum.tile([P, QUAD, QUADS], F32, name="age_bank", tag="pull1")
        for j in range(QUAD):
            nc.tensor.transpose(age_bank[:, j, :], age_col[:, last, j:j + 1].to_broadcast([P, P]), ident[:])
        age_row = half_tile("age_row")
        nc.scalar.copy(age_row[:], age_bank[:])

        keys = [gather(key_words[:].bitcast(U32), U32, f"keys{h}", h * HALF, HALF, f"keys{h}") for h in range(HALVES)]
        score = [product(f"score{h}", pair_codes[:, 0:Q], pair_scale[:, 0:Q], keys[h],
                         key_scale[:, h * HALF:(h + 1) * HALF]) for h in range(HALVES)]
        tangent = [product(f"tangent{h}", pair_codes[:, Q:2 * Q], pair_scale[:, Q:2 * Q], keys[h],
                           key_scale[:, h * HALF:(h + 1) * HALF]) for h in range(HALVES)]

        logit = [half_tile(f"logit{h}") for h in range(HALVES)]
        weight = [half_tile(f"weight{h}") for h in range(HALVES)]
        cool_part = [column(f"cool_part{h}") for h in range(HALVES)]
        for h in range(HALVES):
            nc.vector.tensor_tensor(logit[h][:], score[h], fade[h][:], ALU.subtract)
            nc.scalar.activation(weight[h][:], logit[h][:], ACT.Exp, scale=1.0 / COOL, accum_out=cool_part[h][:])

        gout_codes = shared([P, Q], U32, "gout_codes", "keys0")
        gout_scale = keep.tile([P, Q], U8, name="gout_scale", align_bytes=MX_ALIGN)
        nc.vector.quantize_mx(out=gout_codes[:].bitcast(FP8X4), scales=gout_scale[:],
                              in_=gout_bf[:].rearrange("p q t -> p (q t)"))

        base_sb = shared([P, PAGES], F32, "base_sb", "fade0")
        nc.sync.dma_start(base_sb[:], base)

        cool_sum = shared([P, 1], F32, "cool_sum", "vals1")
        nc.scalar.activation(cool_sum[:], cool_part[0][:], ACT.Identity, bias=cool_part[1][:])
        shift = column("shift")
        nc.scalar.activation(shift[:], cool_sum[:].bitcast(U32), ACT.Copy,
                             scale=-COOL * math.log(2.0) / 2.0 ** 23,
                             bias=COOL * (127.0 * math.log(2.0) + 0.5 * math.log(SLOTS)))
        norm_part = [column(f"norm_part{h}") for h in range(HALVES)]
        for h in range(HALVES):
            nc.scalar.activation(weight[h][:], logit[h][:], ACT.Exp, bias=shift[:], accum_out=norm_part[h][:])
        norm = column("norm")
        nc.scalar.activation(norm[:], norm_part[0][:], ACT.Identity, bias=norm_part[1][:])

        pull = []
        for h, earlier_tenant in enumerate(("fade1", "vals1")):
            vals_h = gather(val_words[:].bitcast(U32), U32, f"vals{h}", h * HALF, HALF, earlier_tenant)
            pull.append(product(f"pull{h}", gout_codes[:], gout_scale[:], vals_h, val_scale[:, h * HALF:(h + 1) * HALF]))

        weight_quads = psum.tile([P, HALVES, QUADS], F32, name="weight_quads", tag="score0")
        for h in range(HALVES):
            aged_quad_sums(weight[h], h, weight_quads[:, h, :], f"weight{h}")

        moved = [half_tile(f"moved{h}") for h in range(HALVES)]
        pulled = [half_tile(f"pulled{h}") for h in range(HALVES)]
        moved_part = [column(f"moved_part{h}") for h in range(HALVES)]
        pulled_part = [column(f"pulled_part{h}") for h in range(HALVES)]
        for h in range(HALVES):
            nc.vector.scalar_tensor_tensor(moved[h][:], weight[h][:], 1.0, tangent[h], ALU.mult, ALU.mult,
                                           accum_out=moved_part[h][:])
        inv_norm = column("inv_norm")
        nc.vector.reciprocal(inv_norm[:], norm[:])
        pulled_quads = psum.tile([P, HALVES, QUADS], F32, name="pulled_quads", tag="score1")
        for h in range(HALVES):
            nc.vector.scalar_tensor_tensor(pulled[h][:], weight[h][:], 1.0, pull[h], ALU.mult, ALU.mult,
                                           accum_out=pulled_part[h][:])
            aged_quad_sums(pulled[h], h, pulled_quads[:, h, :], f"pulled{h}")
        pull_mean = column("pull_mean")
        nc.vector.tensor_scalar(pull_mean[:], pulled_part[0][:], pulled_part[1][:], inv_norm[:], ALU.add, ALU.mult)
        out_factor = column("out_factor")
        nc.vector.tensor_scalar(out_factor[:], inv_norm[:], -OUT_SCALE, None, ALU.mult)
        cov_scale = column("cov_scale")
        nc.vector.tensor_scalar(cov_scale[:], inv_norm[:], -OUT_SCALE, inv_norm[:], ALU.mult, ALU.mult)
        pulled_factor = column("pulled_factor")
        nc.vector.tensor_scalar(pulled_factor[:], moved_part[0][:], moved_part[1][:], cov_scale[:], ALU.add, ALU.mult)

        cross = [half_tile(f"cross{h}") for h in range(HALVES)]
        cross_part = [column(f"cross_part{h}") for h in range(HALVES)]
        cross_quads = psum.tile([P, QUADS], F32, name="cross_quads", tag="tangent0")
        cross_pages = keep.tile([P, PAGES], F32, name="cross_pages")
        for h in range(HALVES):
            nc.vector.scalar_tensor_tensor(cross[h][:], pull[h], pull_mean[:], moved[h][:], ALU.subtract, ALU.mult,
                                           accum_out=cross_part[h][:])
        aged_quad_sums(cross[0], 0, cross_quads[:], "cross0")
        aged_cross = half_tile("aged_cross")
        nc.vector.tensor_tensor(aged_cross[:], cross[last][:], age_row[:], ALU.mult)
        nc.vector.tensor_reduce(cross_pages[:, HALF_PAGES:PAGES],
                                aged_cross[:].rearrange("p j (g r) -> p g j r", r=PAGE_QUADS), AXIS.XY, ALU.add)

        def page_sums(quads, name):
            pages = keep.tile([P, PAGES], F32, name=name)
            nc.vector.tensor_reduce(pages[:], quads[:].rearrange("p h (g r) -> p (h g) r", r=PAGE_QUADS), AXIS.X, ALU.add)
            return pages

        weight_pages = page_sums(weight_quads, "weight_pages")
        cov_factor = column("cov_factor")
        nc.vector.tensor_scalar(cov_factor[:], cross_part[0][:], cross_part[1][:], cov_scale[:], ALU.add, ALU.mult)
        weight_factor = column("weight_factor")
        nc.vector.tensor_scalar(weight_factor[:], pulled_factor[:], pull_mean[:], cov_factor[:], ALU.mult, ALU.subtract)
        with_weight = keep.tile([P, PAGES], F32, name="with_weight")
        nc.vector.scalar_tensor_tensor(with_weight[:], weight_pages[:], weight_factor[:], base_sb[:], ALU.mult, ALU.add)
        pulled_pages = page_sums(pulled_quads, "pulled_pages")
        minus_rest = keep.tile([P, PAGES], F32, name="minus_rest")
        nc.vector.scalar_tensor_tensor(minus_rest[:], pulled_pages[:], pulled_factor[:], with_weight[:],
                                       ALU.mult, ALU.subtract)

        nc.vector.tensor_reduce(cross_pages[:, 0:HALF_PAGES], cross_quads[:].rearrange("p (g r) -> p g r", r=PAGE_QUADS),
                                AXIS.X, ALU.add)
        result = keep.tile([P, PAGES], F32, name="result")
        nc.vector.scalar_tensor_tensor(result[:], cross_pages[:], out_factor[:], minus_rest[:], ALU.mult, ALU.subtract)
        nc.sync.dma_start(out, result[:])
